import numpy as np, ml_dtypes
CORES = [35,38,43,46]
N = 4
import mx_ref
NC, G = 128, 4
C = np.float32(0.031)
BF = ml_dtypes.bfloat16
def cut(t, i, w=512):
    return t[:, w * i:w * i + w]
def tile(rs):
    return np.stack(rs, axis=2).reshape(128, -1).astype(BF)
def layer(w, X):
    out = []
    for i in range(G):
        for t in range(len(X)):
            p = mx_ref.matmul(mx_ref.quantize(cut(w, len(X) * i + t)), X[t])
            z = p if t == 0 else z + p
        out.append(z)
    return out
def act(Z):
    return [np.maximum(z, 0) * C for z in Z]
def pick(b):
    s = np.zeros((128, 128, 4), np.float32)
    s[np.arange(128), np.arange(128), b] = 1.0
    return mx_ref.quantize(s.reshape(128, 512).astype(BF))
def setup_inputs(rng):
    def f(*shape):
        return mx_ref.flush((rng.standard_normal(shape, dtype=np.float32) * np.exp2(rng.integers(-2, 3, shape[:-1] + (1,)))).astype(BF))
    return {"a": f(N, 128, G * 512), "b": f(N, 128, N * 4 * NC), "gr": f(N, 128, N * 4 * NC)}
def setup_inputs_blocks(rng):
    d = setup_inputs(rng)
    for k in ("a", "b", "gr"): d[k] = mx_ref.spread(d[k], rng, 2)
    return d
def setup_inputs_wide(rng):
    d = setup_inputs(rng)
    for k in ("a", "b", "gr"): d[k] = mx_ref.flush((d[k].astype(np.float32) * np.exp2(rng.integers(-4, 5, (N, 1, 1))).astype(np.float32)).astype(BF))
    return d
def setup_inputs_zeros(rng):
    d = setup_inputs(rng); v = d["b"].reshape(N, 128, -1, 4).copy()
    v[np.broadcast_to((rng.random((N, 1, v.shape[2], 1)) < 0.33), v.shape)] = 0
    d["b"] = v.reshape(d["b"].shape)
    return d
def reference(a, b, gr):
    S = [pick(t) for t in range(4)]
    held = lambda q: [mx_ref.matmul(S[t], q) for t in range(4)]
    y = np.zeros((N, 128, NC, 4), np.float32); e = np.zeros((N, N, 128, NC, 4), np.float32)
    for c in range(N):
        for r in range(N):
            R = act(layer(a[r], [mx_ref.quantize(cut(b[r], c, 4 * NC))])); q = mx_ref.quantize(tile(R))
            D = held(q)
            e[r, c] = np.stack([R[t] - D[t] for t in range(4)], axis=2)
            p = np.stack(D if r == c else held(q), axis=2)
            q2 = mx_ref.quantize((cut(gr[r], c, 4 * NC).astype(np.float32) + e[r, c].reshape(128, -1)).astype(BF))
            p = p + np.stack(held(q2), axis=2)
            y[c] = p if r == 0 else y[c] + p
    return {"y": y.reshape(N, 128, 4 * NC)}

@@ -1,0 +1,285 @@
+from concourse.bass import DstId, RemoteDMATransfer
+from concourse.mybir import dt, AluOpType, ActivationFunctionType
+
+C = 0.031
+NC = 128
+W = 4 * NC
+CODES = "float8_e4m3fn_x4"
+
+SCRATCH = {
+    "pick": ("sbuf", [128, 520], "bfloat16"),
+    "ra": ("sbuf", [128, 2048], "bfloat16"),
+    "rb": ("sbuf", [128, 2048], "bfloat16"),
+    "rg": ("sbuf", [128, 2048], "bfloat16"),
+    "t": ("sbuf", [128, 2048], "bfloat16"),
+    "u": ("sbuf", [128, 2048], "bfloat16"),
+    "rf": ("sbuf", [128, 2048], "float32"),
+    "ef": ("sbuf", [128, 2048], "float32"),
+    "dc": ("sbuf", [128, 512], "float32"),
+    "yo": ("sbuf", [128, 512], "float32"),
+    "px": ("psum", [128, 2048], "float32"),
+    "py": ("psum", [128, 2048], "float32"),
+}
+for _n in ("qs", "qa", "qb", "q", "qu", "lq", "lu"):
+    SCRATCH[_n] = ("sbuf", [128, 512], CODES)
+    SCRATCH[_n + "_s"] = ("sbuf", [128, 512], "uint8")
+
+LOADS = ["la0", "la1", "lb0", "lb1", "lg0", "lg1"]
+SEMAPHORES = LOADS + ["sv", "sa", "sp", "sg", "sent", "sy"] + ["aq%d" % r for r in range(4)] + ["au%d" % r for r in range(4)]
+
+
+def engines(m):
+    return [e for e in range(m.bit_length()) if (m >> e) & 1]
+
+
+def mask_of(es):
+    return sum(1 << e for e in es)
+
+
+def plan(rank, cores, topo):
+    me = cores[rank]
+    others = [c for c in range(len(cores)) if c != rank]
+    others.sort(key=lambda c: (topo.chip(cores[c]) == topo.chip(me), topo.die(cores[c]) != topo.die(me)))
+    c1, c2, c3 = others
+    off = engines(topo.mask(me, cores[c1]))
+    on = engines(topo.mask(me, cores[c3]))
+    rest = [e for e in on if e not in off]
+    h = len(off) // 2
+    m = {("q", c1): off, ("q", c2): off, ("q", c3): rest,
+         ("q_s", c1): off[:h], ("q_s", c2): off[h:], ("q_s", c3): rest,
+         ("u", c1): off, ("u", c2): off, ("u", c3): on,
+         ("u_s", c1): off, ("u_s", c2): off, ("u_s", c3): on}
+    return others + [rank], {k: mask_of(v) for k, v in m.items()}
+
+
+def rank_program(g, core, T, topo):
+    rank = T.rank_of(core)
+    if rank is None:
+        return
+    cores = list(T.cores)
+    order, masks = plan(rank, cores, topo)
+    c1, c2, c3, own = order
+    S = T.sem
+    A = ActivationFunctionType
+    queues = {"v": g.vector, "a": g.scalar, "t": g.tensor, "g": g, "s": g.sync}
+    counter = {"v": "sv", "a": "sa", "t": "sp"}
+    ops = {k: [] for k in queues}
+    at = {}
+    count = {k: 0 for k in queues}
+
+    def add(eng, label, deps, call, counted=True):
+        if counted:
+            count[eng] += 1
+            at[label] = (counter[eng], count[eng])
+        ops[eng].append((deps, call, counted))
+
+    def codes(buf, c, n=NC):
+        return T[buf][:, c * NC:c * NC + n]
+
+    def plane(buf, c, n=NC):
+        return T[buf + "_s"][:, c * NC:c * NC + n]
+
+    def bank(buf, b, off=0, n=NC):
+        return T[buf][:, b * 512 + off:b * 512 + off + n]
+
+    def comb(buf, c, b):
+        return T[buf][:, c * W + b:(c + 1) * W:4]
+
+    def flat(buf, c, b):
+        return T[buf][:, c * W + b * NC:c * W + (b + 1) * NC]
+
+    far = min(c1, c2)
+    near = min(c3, own)
+
+    def load(eng, sem, dst, src, lo):
+        add(eng, sem, [], lambda: queues[eng].dma_start(dst[:, lo:lo + 1024], src[:, lo:lo + 1024]).then_inc(S[sem], 16), False)
+
+    load("s", "la0", T.ra, T.a, 0)
+    load("a", "la1", T.ra, T.a, 1024)
+    load("s", "lb0", T.rb, T.b, far * W)
+    load("a", "lb1", T.rb, T.b, near * W)
+    load("s", "lg0", T.rg, T.gr, far * W)
+    load("s", "lg1", T.rg, T.gr, near * W)
+    L = {k: (k, 16) for k in LOADS}
+
+    add("v", "ones", [], lambda: g.vector.memset(T.pick[:, 0:515], 1.0))
+    add("g", "sel", ["ones"], lambda: g.affine_select(T.pick[:, 0:515], T.pick[:, 0:515], [[-1, 515]], AluOpType.is_equal, 0.0, 3, 4).then_inc(S.sg, 1), False)
+
+    def quant(label, deps, buf, c, src, lo, n=NC):
+        add("v", label, deps, lambda: g.vector.quantize_mx(codes(buf, c, n), plane(buf, c, n), T[src][:, lo:lo + 4 * n]))
+
+    for b in range(4):
+        quant("S%d" % b, [("sg", 1)], "qs", b, "pick", 3 - b)
+
+    def relu_v(label, deps, out, in_):
+        add("v", label, deps, lambda: g.vector.tensor_scalar(out, in_, 0.0, C, AluOpType.max, AluOpType.mult))
+
+    def relu_a(label, deps, out, in_):
+        add("a", label, deps, lambda: g.scalar.activation(out, in_, A.Relu, scale=C))
+
+    def mm(label, deps, out, w, i, x, c, n=NC, start=True, stop=True):
+        add("t", label, deps, lambda: g.tensor.matmul_mx(out, codes(w, i), plane(w, i), codes(x, c, n), plane(x, c, n), start, stop))
+
+    quant("qa0", [L["la0"]], "qa", 0, "ra", 0, 256)
+    quant("qa1", [L["la1"]], "qa", 2, "ra", 1024, 256)
+    quant("qb0", [L["lb0"]], "qb", c1, "rb", c1 * W)
+    quant("qb1", [L["lb0"]], "qb", c2, "rb", c2 * W)
+
+    zbuf = {c1: ("px", 0), c2: ("py", 0), c3: ("py", (c3 - near) * NC), own: ("py", (own - near) * NC)}
+    zlab = {c1: "Z0_%d", c2: "Z1_%d", c3: "Z2_%d", own: "Z2_%d"}
+
+    def zbank(c, i):
+        return bank(zbuf[c][0], i, zbuf[c][1])
+
+    def make(which, eng, c, i, deps=()):
+        out = comb("t", c, i) if which == "P" else flat("rf", c, i)
+        (relu_v if eng == "v" else relu_a)("%s%d_%d" % (which, c, i), [zlab[c] % i] + list(deps), out, zbank(c, i))
+
+    BO = {0: (2, 3, 0, 1), 1: (0, 1, 2, 3), 2: (0, 1, 2, 3), 3: (0, 1, 2, 3)}
+
+    def qtile(c):
+        quant("q%d" % c, ["P%d_%d" % (c, i) for i in range(4)], "q", c, "t", c * W)
+
+    def second(k):
+        c = order[k]
+        bs = BO[k]
+
+        def e(b):
+            add("v", "E%d_%d" % (k, b), ["D%d_%d" % (k, b), "F%d_%d" % (c, b)],
+                lambda: g.vector.tensor_tensor(flat("ef", c, b), flat("rf", c, b), bank("px", b), AluOpType.subtract))
+
+        def u(b):
+            add("v", "u%d_%d" % (k, b), ["E%d_%d" % (k, b), L["lg0" if k < 2 else "lg1"]],
+                lambda: g.vector.tensor_tensor(comb("u", c, b), comb("rg", c, b), flat("ef", c, b), AluOpType.add))
+
+        e(bs[0])
+        for j in range(1, 4):
+            e(bs[j])
+            u(bs[j - 1])
+        u(bs[3])
+
+    def qsecond(k):
+        c = order[k]
+        quant("qu%d" % k, ["u%d_%d" % (k, b) for b in range(4)], "qu", c, "u", c * W)
+
+    for i in (0, 1):
+        make("P", "v", c1, i)
+    qtile(c1)
+    for i in range(4):
+        make("P", "v", c2, i)
+    qtile(c2)
+    quant("qb2", [L["lb1"]], "qb", near, "rb", near * W, 256)
+    second(0)
+    qtile(c3)
+    qsecond(0)
+    second(1)
+    qtile(own)
+    qsecond(1)
+    second(2)
+    qsecond(2)
+    second(3)
+    qsecond(3)
+    for b in range(4):
+        add("v", "y%d" % b, ["U2_%d" % b, "dc%d" % b],
+            (lambda b: lambda: g.vector.tensor_tensor(T.yo[:, b:512:4], bank("py", b), T.dc[:, b * NC:(b + 1) * NC], AluOpType.add))(b))
+
+    for i in (2, 3):
+        make("P", "a", c1, i)
+    for i in BO[0]:
+        make("F", "a", c1, i, ["P%d_%d" % (c1, i)])
+    for i in range(4):
+        make("F", "a", c2, i, ["P%d_%d" % (c2, i)])
+    for c in (c3, own):
+        for i in range(4):
+            make("P", "a", c, i)
+        for i in range(4):
+            make("F", "a", c, i)
+    for b in BO[3]:
+        add("a", "dc%d" % b, ["E3_%d" % b], (lambda b: lambda: g.scalar.activation(T.dc[:, b * NC:(b + 1) * NC], bank("px", b), A.Copy))(b))
+
+    for i in BO[0]:
+        mm("Z0_%d" % i, ["qa%d" % (i // 2), "qb0"], bank("px", i), "qa", i, "qb", c1)
+    for i in range(4):
+        mm("Z1_%d" % i, ["qa%d" % (i // 2), "qb1"], bank("py", i), "qa", i, "qb", c2)
+
+    def held(k, free):
+        for b in BO[k]:
+            mm("D%d_%d" % (k, b), ["S%d" % b, "q%d" % order[k]] + free(b), bank("px", b), "qs", b, "q", order[k])
+
+    held(0, lambda b: ["F%d_%d" % (c1, b), "P%d_%d" % (c1, b)])
+    for i in range(4):
+        mm("Z2_%d" % i, ["qb2", "F%d_%d" % (c2, i), "P%d_%d" % (c2, i)], bank("py", i, 0, 256), "qa", i, "qb", near, 256)
+    for k in (1, 2, 3):
+        held(k, lambda b: ["E%d_%d" % (k - 1, b)])
+
+    def total(src, what):
+        m = plan(src, cores, topo)[1]
+        return len(engines(m[(what, rank)])) + len(engines(m[(what + "_s", rank)]))
+
+    for j in range(3):
+        src = order[j]
+        for b in range(4):
+            mm("A%d_%d" % (j, b), [("aq%d" % src, total(src, "q")), "F%d_%d" % (c3, b), "F%d_%d" % (own, b)],
+               bank("py", b), "qs", b, "lq", src, start=(j == 0), stop=False)
+    for j in (0, 1, 3, 2):
+        src = order[j]
+        for b in range(4):
+            dep = ["qu3"] if j == 3 else [("au%d" % src, total(src, "u"))]
+            mm("U%d_%d" % (j, b), dep, bank("py", b), "qs", b, "qu" if j == 3 else "lu", src, start=False, stop=(j == 2))
+
+    sent = [0]
+
+    def dest(c):
+        rid, pid, _se = topo.addr(cores[c])
+        return rid, pid
+
+    def piece(kind, c):
+        src = {"q": "q", "u": "qu"}[kind[0]]
+        land = {"q": "lq", "u": "lu"}[kind[0]]
+        if kind.endswith("_s"):
+            return plane(src, c), plane(land, rank)
+        return codes(src, c).bitcast(dt.uint8), codes(land, rank).bitcast(dt.uint8)
+
+    def send(deps, items):
+        def call():
+            tr = []
+            for kind, c in items:
+                rid, pid = dest(c)
+                s, d = piece(kind, c)
+                tr.append((rid, pid, s, d, masks[(kind, c)], S["a%s%d" % (kind[0], rank)]))
+            if len(tr) == 1:
+                rid, pid, s, d, m, sem = tr[0]
+                g.remote_dma(d, s, sem, S.sent, pid, rid, m)
+            else:
+                g.remote_dma_fused([RemoteDMATransfer(dst_ids=[DstId(rid=rid, pnc=pid)], dma_engine_mask=m, remote_sem=sem, src=s, dst=d)
+                                    for rid, pid, s, d, m, sem in tr], local_sem=S.sent)
+        for kind, c in items:
+            sent[0] += len(engines(masks[(kind, c)]))
+        add("g", None, deps, call, False)
+
+    send(["q%d" % c1], [("q", c1)])
+    send(["q%d" % c2, "q%d" % c3], [("q", c2), ("q", c3)])
+    send([], [("q_s", c1), ("q_s", c2), ("q_s", c3)])
+    for k in range(3):
+        send(["qu%d" % k], [("u", order[k])])
+        send([], [("u_s", order[k])])
+
+    add("s", None, ["y%d" % b for b in range(4)], lambda: g.sync.dma_start(T.y[:], T.yo[:]).then_inc(S.sy, 16), False)
+
+    for eng in ops:
+        q = queues[eng]
+        seen = {}
+        for deps, call, counted in ops[eng]:
+            need = {}
+            for d in deps:
+                s, n = at[d] if isinstance(d, str) else d
+                need[s] = max(need.get(s, 0), n)
+            for s, n in need.items():
+                if seen.get(s, 0) < n:
+                    q.wait_ge(S[s], n)
+                    seen[s] = n
+            ins = call()
+            if counted:
+                ins.then_inc(S[counter[eng]], 1)
+    g.sync.wait_ge(S.sy, 16)
+    g.wait_ge(S.sent, sent[0])

@@ -7,6 +7,7 @@ W = 4 * NC
 CODES = "float8_e4m3fn_x4"
 
 SCRATCH = {
+    "one": ("sbuf", [128, 128], "bfloat16"),
     "pick": ("sbuf", [128, 520], "bfloat16"),
     "ra": ("sbuf", [128, 2048], "bfloat16"),
     "rb": ("sbuf", [128, 2048], "bfloat16"),
@@ -24,8 +25,8 @@ for _n in ("qs", "qa", "qb", "q", "qu", "lq", "lu"):
     SCRATCH[_n] = ("sbuf", [128, 512], CODES)
     SCRATCH[_n + "_s"] = ("sbuf", [128, 512], "uint8")
 
-LOADS = ["la0", "la1", "lb0", "lb1", "lg0", "lg1"]
-SEMAPHORES = LOADS + ["sv", "sa", "sp", "sg", "sent", "sy"] + ["aq%d" % r for r in range(4)] + ["au%d" % r for r in range(4)]
+LOADS = ["la0", "la1", "lb0", "lb1", "lb2", "lg0", "lg1"]
+SEMAPHORES = LOADS + ["sv", "sa", "sp", "sg", "sent", "sy0", "sy1"] + ["aq%d" % r for r in range(4)] + ["au%d" % r for r in range(4)]
 
 
 def engines(m):
@@ -40,15 +41,15 @@ def plan(rank, cores, topo):
     me = cores[rank]
     others = [c for c in range(len(cores)) if c != rank]
     others.sort(key=lambda c: (topo.chip(cores[c]) == topo.chip(me), topo.die(cores[c]) != topo.die(me)))
-    c1, c2, c3 = others
-    off = engines(topo.mask(me, cores[c1]))
-    on = engines(topo.mask(me, cores[c3]))
+    f1, f2, x = others
+    off = engines(topo.mask(me, cores[f1]))
+    on = engines(topo.mask(me, cores[x]))
     rest = [e for e in on if e not in off]
     h = len(off) // 2
-    m = {("q", c1): off, ("q", c2): off, ("q", c3): rest,
-         ("q_s", c1): off[:h], ("q_s", c2): off[h:], ("q_s", c3): rest,
-         ("u", c1): off, ("u", c2): off, ("u", c3): on,
-         ("u_s", c1): off, ("u_s", c2): off, ("u_s", c3): on}
+    m = {("q", f1): off, ("q", f2): off, ("q", x): rest,
+         ("q_s", f1): off[:h], ("q_s", f2): off[h:], ("q_s", x): rest,
+         ("u", f1): off, ("u", f2): off, ("u", x): on,
+         ("u_s", f1): off, ("u_s", f2): off, ("u_s", x): on}
     return others + [rank], {k: mask_of(v) for k, v in m.items()}
 
 
@@ -58,7 +59,7 @@ def rank_program(g, core, T, topo):
         return
     cores = list(T.cores)
     order, masks = plan(rank, cores, topo)
-    c1, c2, c3, own = order
+    f1, f2, x, own = order
     S = T.sem
     A = ActivationFunctionType
     queues = {"v": g.vector, "a": g.scalar, "t": g.tensor, "g": g, "s": g.sync}
@@ -88,22 +89,24 @@ def rank_program(g, core, T, topo):
     def flat(buf, c, b):
         return T[buf][:, c * W + b * NC:c * W + (b + 1) * NC]
 
-    far = min(c1, c2)
-    near = min(c3, own)
+    far = min(f1, f2)
+    near = min(x, own)
 
-    def load(eng, sem, dst, src, lo):
-        add(eng, sem, [], lambda: queues[eng].dma_start(dst[:, lo:lo + 1024], src[:, lo:lo + 1024]).then_inc(S[sem], 16), False)
+    def load(eng, sem, dst, src, lo, n=1024):
+        add(eng, None, [], lambda: queues[eng].dma_start(dst[:, lo:lo + n], src[:, lo:lo + n]).then_inc(S[sem], 16), False)
 
-    load("s", "la0", T.ra, T.a, 0)
-    load("a", "la1", T.ra, T.a, 1024)
-    load("s", "lb0", T.rb, T.b, far * W)
-    load("a", "lb1", T.rb, T.b, near * W)
+    load("s", "lb0", T.rb, T.b, f1 * W, W)
+    load("a", "la0", T.ra, T.a, 0)
+    load("s", "la1", T.ra, T.a, 1024)
+    load("s", "lb1", T.rb, T.b, f2 * W, W)
+    load("a", "lb2", T.rb, T.b, near * W)
     load("s", "lg0", T.rg, T.gr, far * W)
     load("s", "lg1", T.rg, T.gr, near * W)
     L = {k: (k, 16) for k in LOADS}
 
-    add("v", "ones", [], lambda: g.vector.memset(T.pick[:, 0:515], 1.0))
-    add("g", "sel", ["ones"], lambda: g.affine_select(T.pick[:, 0:515], T.pick[:, 0:515], [[-1, 515]], AluOpType.is_equal, 0.0, 3, 4).then_inc(S.sg, 1), False)
+    add("v", "one", [], lambda: g.vector.memset(T.one[:], 1.0))
+    add("v", "zero", [], lambda: g.vector.memset(T.pick[:, 0:520], 0.0))
+    add("g", None, ["zero"], lambda: g.affine_select(T.pick[:, 3:515:4], T.one[:], [[-1, 128]], AluOpType.is_equal, 0.0, 0, 1).then_inc(S.sg, 1), False)
 
     def quant(label, deps, buf, c, src, lo, n=NC):
         add("v", label, deps, lambda: g.vector.quantize_mx(codes(buf, c, n), plane(buf, c, n), T[src][:, lo:lo + 4 * n]))
@@ -117,115 +120,106 @@ def rank_program(g, core, T, topo):
     def relu_a(label, deps, out, in_):
         add("a", label, deps, lambda: g.scalar.activation(out, in_, A.Relu, scale=C))
 
-    def mm(label, deps, out, w, i, x, c, n=NC, start=True, stop=True):
-        add("t", label, deps, lambda: g.tensor.matmul_mx(out, codes(w, i), plane(w, i), codes(x, c, n), plane(x, c, n), start, stop))
+    def mm(label, deps, out, w, i, m, c, n=NC, start=True, stop=True):
+        add("t", label, deps, lambda: g.tensor.matmul_mx(out, codes(w, i), plane(w, i), codes(m, c, n), plane(m, c, n), start, stop))
 
-    quant("qa0", [L["la0"]], "qa", 0, "ra", 0, 256)
-    quant("qa1", [L["la1"]], "qa", 2, "ra", 1024, 256)
-    quant("qb0", [L["lb0"]], "qb", c1, "rb", c1 * W)
-    quant("qb1", [L["lb0"]], "qb", c2, "rb", c2 * W)
-
-    zbuf = {c1: ("px", 0), c2: ("py", 0), c3: ("py", (c3 - near) * NC), own: ("py", (own - near) * NC)}
-    zlab = {c1: "Z0_%d", c2: "Z1_%d", c3: "Z2_%d", own: "Z2_%d"}
-
-    def zbank(c, i):
-        return bank(zbuf[c][0], i, zbuf[c][1])
+    zbuf = {f1: ("px", 0), f2: ("py", 0), x: ("py", (x - near) * NC), own: ("py", (own - near) * NC)}
+    zlab = {f1: "Z1_%d", f2: "Z2_%d", x: "ZN_%d", own: "ZN_%d"}
 
     def make(which, eng, c, i, deps=()):
         out = comb("t", c, i) if which == "P" else flat("rf", c, i)
-        (relu_v if eng == "v" else relu_a)("%s%d_%d" % (which, c, i), [zlab[c] % i] + list(deps), out, zbank(c, i))
-
-    BO = {0: (2, 3, 0, 1), 1: (0, 1, 2, 3), 2: (0, 1, 2, 3), 3: (0, 1, 2, 3)}
+        (relu_v if eng == "v" else relu_a)("%s%d_%d" % (which, c, i), [zlab[c] % i] + list(deps), out, bank(zbuf[c][0], i, zbuf[c][1]))
 
     def qtile(c):
         quant("q%d" % c, ["P%d_%d" % (c, i) for i in range(4)], "q", c, "t", c * W)
 
-    def second(k):
-        c = order[k]
-        bs = BO[k]
-
+    def second(c):
         def e(b):
-            add("v", "E%d_%d" % (k, b), ["D%d_%d" % (k, b), "F%d_%d" % (c, b)],
+            add("v", "E%d_%d" % (c, b), ["D%d_%d" % (c, b), "F%d_%d" % (c, b)],
                 lambda: g.vector.tensor_tensor(flat("ef", c, b), flat("rf", c, b), bank("px", b), AluOpType.subtract))
 
         def u(b):
-            add("v", "u%d_%d" % (k, b), ["E%d_%d" % (k, b), L["lg0" if k < 2 else "lg1"]],
+            add("v", "u%d_%d" % (c, b), ["E%d_%d" % (c, b), L["lg0" if c in (f1, f2) else "lg1"]],
                 lambda: g.vector.tensor_tensor(comb("u", c, b), comb("rg", c, b), flat("ef", c, b), AluOpType.add))
 
-        e(bs[0])
-        for j in range(1, 4):
-            e(bs[j])
-            u(bs[j - 1])
-        u(bs[3])
+        e(0)
+        for b in range(1, 4):
+            e(b)
+            u(b - 1)
+        u(3)
 
-    def qsecond(k):
-        c = order[k]
-        quant("qu%d" % k, ["u%d_%d" % (k, b) for b in range(4)], "qu", c, "u", c * W)
+    def qsecond(c):
+        quant("qu%d" % c, ["u%d_%d" % (c, b) for b in range(4)], "qu", c, "u", c * W)
 
+    quant("qb%d" % f1, [L["lb0"]], "qb", f1, "rb", f1 * W)
+    for i in range(4):
+        quant("qa%d" % i, [L["la%d" % (i // 2)]], "qa", i, "ra", i * W)
+    quant("qb%d" % f2, [L["lb1"]], "qb", f2, "rb", f2 * W)
+    make("P", "v", f1, 3)
+    qtile(f1)
     for i in (0, 1):
-        make("P", "v", c1, i)
-    qtile(c1)
-    for i in range(4):
-        make("P", "v", c2, i)
-    qtile(c2)
-    quant("qb2", [L["lb1"]], "qb", near, "rb", near * W, 256)
-    second(0)
-    qtile(c3)
-    qsecond(0)
-    second(1)
+        make("P", "v", f2, i)
+    quant("qbn", [L["lb2"]], "qb", near, "rb", near * W, 256)
+    qtile(f2)
+    second(f1)
+    qtile(x)
+    qsecond(f1)
+    second(f2)
     qtile(own)
-    qsecond(1)
-    second(2)
-    qsecond(2)
-    second(3)
-    qsecond(3)
-    for b in range(4):
-        add("v", "y%d" % b, ["U2_%d" % b, "dc%d" % b],
-            (lambda b: lambda: g.vector.tensor_tensor(T.yo[:, b:512:4], bank("py", b), T.dc[:, b * NC:(b + 1) * NC], AluOpType.add))(b))
+    qsecond(f2)
+    second(x)
+    qsecond(x)
+    second(own)
+    qsecond(own)
+    for h in range(2):
+        for b in range(4):
+            add("v", "y%d_%d" % (h, b), ["UX_%d" % b, "dc%d" % b],
+                (lambda b, lo: lambda: g.vector.tensor_tensor(T.yo[:, 4 * lo + b:4 * lo + 256:4], bank("py", b, lo, 64), T.dc[:, b * NC + lo:b * NC + lo + 64], AluOpType.add))(b, 64 * h))
 
-    for i in (2, 3):
-        make("P", "a", c1, i)
-    for i in BO[0]:
-        make("F", "a", c1, i, ["P%d_%d" % (c1, i)])
+    for i in (0, 1, 2):
+        make("P", "a", f1, i)
     for i in range(4):
-        make("F", "a", c2, i, ["P%d_%d" % (c2, i)])
-    for c in (c3, own):
+        make("F", "a", f1, i, ["P%d_%d" % (f1, i)])
+    for i in (2, 3):
+        make("P", "a", f2, i)
+    for i in range(4):
+        make("F", "a", f2, i, ["P%d_%d" % (f2, i)])
+    for c in (x, own):
         for i in range(4):
             make("P", "a", c, i)
         for i in range(4):
             make("F", "a", c, i)
-    for b in BO[3]:
-        add("a", "dc%d" % b, ["E3_%d" % b], (lambda b: lambda: g.scalar.activation(T.dc[:, b * NC:(b + 1) * NC], bank("px", b), A.Copy))(b))
+    for b in range(4):
+        add("a", "dc%d" % b, ["E%d_%d" % (own, b)], (lambda b: lambda: g.scalar.activation(T.dc[:, b * NC:(b + 1) * NC], bank("px", b), A.Copy))(b))
 
-    for i in BO[0]:
-        mm("Z0_%d" % i, ["qa%d" % (i // 2), "qb0"], bank("px", i), "qa", i, "qb", c1)
     for i in range(4):
-        mm("Z1_%d" % i, ["qa%d" % (i // 2), "qb1"], bank("py", i), "qa", i, "qb", c2)
-
-    def held(k, free):
-        for b in BO[k]:
-            mm("D%d_%d" % (k, b), ["S%d" % b, "q%d" % order[k]] + free(b), bank("px", b), "qs", b, "q", order[k])
-
-    held(0, lambda b: ["F%d_%d" % (c1, b), "P%d_%d" % (c1, b)])
+        mm("Z1_%d" % i, ["qa%d" % i, "qb%d" % f1], bank("px", i), "qa", i, "qb", f1)
     for i in range(4):
-        mm("Z2_%d" % i, ["qb2", "F%d_%d" % (c2, i), "P%d_%d" % (c2, i)], bank("py", i, 0, 256), "qa", i, "qb", near, 256)
-    for k in (1, 2, 3):
-        held(k, lambda b: ["E%d_%d" % (k - 1, b)])
+        mm("Z2_%d" % i, ["qb%d" % f2], bank("py", i), "qa", i, "qb", f2)
+
+    def held(c, free):
+        for b in range(4):
+            mm("D%d_%d" % (c, b), ["S%d" % b, "q%d" % c] + [f % b for f in free], bank("px", b), "qs", b, "q", c)
+
+    held(f1, ["F%d_%%d" % f1, "P%d_%%d" % f1])
+    for i in range(4):
+        mm("ZN_%d" % i, ["qbn", "F%d_%d" % (f2, i), "P%d_%d" % (f2, i)], bank("py", i, 0, 256), "qa", i, "qb", near, 256)
+    held(f2, ["E%d_%%d" % f1])
+    held(x, ["E%d_%%d" % f2])
+    held(own, ["E%d_%%d" % x])
 
     def total(src, what):
         m = plan(src, cores, topo)[1]
         return len(engines(m[(what, rank)])) + len(engines(m[(what + "_s", rank)]))
 
-    for j in range(3):
-        src = order[j]
+    for j, src in enumerate((f1, f2, x)):
         for b in range(4):
-            mm("A%d_%d" % (j, b), [("aq%d" % src, total(src, "q")), "F%d_%d" % (c3, b), "F%d_%d" % (own, b)],
+            mm("A%d_%d" % (j, b), [("aq%d" % src, total(src, "q"))] + ["%s%d_%d" % (k, c, b) for k in "PF" for c in (x, own)],
                bank("py", b), "qs", b, "lq", src, start=(j == 0), stop=False)
-    for j in (0, 1, 3, 2):
-        src = order[j]
+    for src in (f1, f2, own, x):
         for b in range(4):
-            dep = ["qu3"] if j == 3 else [("au%d" % src, total(src, "u"))]
-            mm("U%d_%d" % (j, b), dep, bank("py", b), "qs", b, "qu" if j == 3 else "lu", src, start=False, stop=(j == 2))
+            dep = ["qu%d" % own] if src == own else [("au%d" % src, total(src, "u"))]
+            mm("UX_%d" % b if src == x else "U%d_%d" % (src, b), dep, bank("py", b), "qs", b, "qu" if src == own else "lu", src, start=False, stop=(src == x))
 
     sent = [0]
 
@@ -257,14 +251,16 @@ def rank_program(g, core, T, topo):
             sent[0] += len(engines(masks[(kind, c)]))
         add("g", None, deps, call, False)
 
-    send(["q%d" % c1], [("q", c1)])
-    send(["q%d" % c2, "q%d" % c3], [("q", c2), ("q", c3)])
-    send([], [("q_s", c1), ("q_s", c2), ("q_s", c3)])
-    for k in range(3):
-        send(["qu%d" % k], [("u", order[k])])
-        send([], [("u_s", order[k])])
+    send(["q%d" % f1], [("q", f1)])
+    send(["q%d" % f2, "q%d" % x], [("q", f2), ("q", x)])
+    send([], [("q_s", f1), ("q_s", f2), ("q_s", x)])
+    for c in (f1, f2, x):
+        send(["qu%d" % c], [("u", c)])
+        send([], [("u_s", c)])
 
-    add("s", None, ["y%d" % b for b in range(4)], lambda: g.sync.dma_start(T.y[:], T.yo[:]).then_inc(S.sy, 16), False)
+    for h in range(2):
+        add("s", None, ["y%d_%d" % (h, b) for b in range(4)],
+            (lambda h: lambda: g.sync.dma_start(T.y[:, 256 * h:256 * h + 256], T.yo[:, 256 * h:256 * h + 256]).then_inc(S["sy%d" % h], 16))(h), False)
 
     for eng in ops:
         q = queues[eng]
@@ -281,5 +277,6 @@ def rank_program(g, core, T, topo):
             ins = call()
             if counted:
                 ins.then_inc(S[counter[eng]], 1)
-    g.sync.wait_ge(S.sy, 16)
+    g.sync.wait_ge(S.sy0, 16)
+    g.sync.wait_ge(S.sy1, 16)
     g.wait_ge(S.sent, sent[0])

@@ -25,7 +25,7 @@ for _n in ("qs", "qa", "qb", "q", "qu", "lq", "lu"):
     SCRATCH[_n] = ("sbuf", [128, 512], CODES)
     SCRATCH[_n + "_s"] = ("sbuf", [128, 512], "uint8")
 
-LOADS = ["la0", "la1", "lb0", "lb1", "lb2", "lg0", "lg1"]
+LOADS = ["la0", "la1", "la2", "lb0", "lb1", "lb2", "lg0", "lg1", "lg2"]
 SEMAPHORES = LOADS + ["sv", "sa", "sp", "sg", "sent", "sy0", "sy1"] + ["aq%d" % r for r in range(4)] + ["au%d" % r for r in range(4)]
 
 
@@ -89,20 +89,22 @@ def rank_program(g, core, T, topo):
     def flat(buf, c, b):
         return T[buf][:, c * W + b * NC:c * W + (b + 1) * NC]
 
-    far = min(f1, f2)
     near = min(x, own)
 
-    def load(eng, sem, dst, src, lo, n=1024):
+    def load(eng, sem, dst, src, lo, n=W):
         add(eng, None, [], lambda: queues[eng].dma_start(dst[:, lo:lo + n], src[:, lo:lo + n]).then_inc(S[sem], 16), False)
 
-    load("s", "lb0", T.rb, T.b, f1 * W, W)
-    load("a", "la0", T.ra, T.a, 0)
-    load("s", "la1", T.ra, T.a, 1024)
-    load("s", "lb1", T.rb, T.b, f2 * W, W)
-    load("a", "lb2", T.rb, T.b, near * W)
-    load("s", "lg0", T.rg, T.gr, far * W)
-    load("s", "lg1", T.rg, T.gr, near * W)
+    load("s", "lb0", T.rb, T.b, f1 * W)
+    load("a", "la0", T.ra, T.a, 0, 2 * W)
+    load("s", "la1", T.ra, T.a, 2 * W)
+    load("a", "la2", T.ra, T.a, 3 * W)
+    load("s", "lb1", T.rb, T.b, f2 * W)
+    load("s", "lb2", T.rb, T.b, near * W, 2 * W)
+    load("s", "lg0", T.rg, T.gr, f1 * W)
+    load("s", "lg2", T.rg, T.gr, f2 * W)
+    load("s", "lg1", T.rg, T.gr, near * W, 2 * W)
     L = {k: (k, 16) for k in LOADS}
+    gload = {f1: L["lg0"], f2: L["lg2"], x: L["lg1"], own: L["lg1"]}
 
     add("v", "one", [], lambda: g.vector.memset(T.one[:], 1.0))
     add("v", "zero", [], lambda: g.vector.memset(T.pick[:, 0:520], 0.0))
@@ -114,38 +116,35 @@ def rank_program(g, core, T, topo):
     for b in range(4):
         quant("S%d" % b, [("sg", 1)], "qs", b, "pick", 3 - b)
 
-    def relu_v(label, deps, out, in_):
-        add("v", label, deps, lambda: g.vector.tensor_scalar(out, in_, 0.0, C, AluOpType.max, AluOpType.mult))
-
-    def relu_a(label, deps, out, in_):
-        add("a", label, deps, lambda: g.scalar.activation(out, in_, A.Relu, scale=C))
-
     def mm(label, deps, out, w, i, m, c, n=NC, start=True, stop=True):
         add("t", label, deps, lambda: g.tensor.matmul_mx(out, codes(w, i), plane(w, i), codes(m, c, n), plane(m, c, n), start, stop))
 
-    zbuf = {f1: ("px", 0), f2: ("py", 0), x: ("py", (x - near) * NC), own: ("py", (own - near) * NC)}
+    zbuf = {f1: ("px", 0), f2: ("py", 0), x: ("px", (x - near) * NC), own: ("px", (own - near) * NC)}
     zlab = {f1: "Z1_%d", f2: "Z2_%d", x: "ZN_%d", own: "ZN_%d"}
+    dbuf = {f1: "px", f2: "py", x: "py", own: "py"}
 
-    def make(which, eng, c, i, deps=()):
+    def make(which, c, i):
         out = comb("t", c, i) if which == "P" else flat("rf", c, i)
-        (relu_v if eng == "v" else relu_a)("%s%d_%d" % (which, c, i), [zlab[c] % i] + list(deps), out, bank(zbuf[c][0], i, zbuf[c][1]))
+        add("a", "%s%d_%d" % (which, c, i), [zlab[c] % i], lambda: g.scalar.activation(out, bank(zbuf[c][0], i, zbuf[c][1]), A.Relu, scale=C))
 
     def qtile(c):
         quant("q%d" % c, ["P%d_%d" % (c, i) for i in range(4)], "q", c, "t", c * W)
 
-    def second(c):
+    def second(c, fill):
         def e(b):
             add("v", "E%d_%d" % (c, b), ["D%d_%d" % (c, b), "F%d_%d" % (c, b)],
-                lambda: g.vector.tensor_tensor(flat("ef", c, b), flat("rf", c, b), bank("px", b), AluOpType.subtract))
+                lambda: g.vector.tensor_tensor(flat("ef", c, b), flat("rf", c, b), bank(dbuf[c], b), AluOpType.subtract))
 
         def u(b):
-            add("v", "u%d_%d" % (c, b), ["E%d_%d" % (c, b), L["lg0" if c in (f1, f2) else "lg1"]],
+            add("v", "u%d_%d" % (c, b), ["E%d_%d" % (c, b), gload[c]],
                 lambda: g.vector.tensor_tensor(comb("u", c, b), comb("rg", c, b), flat("ef", c, b), AluOpType.add))
 
-        e(0)
-        for b in range(1, 4):
+        for b in range(4):
             e(b)
-            u(b - 1)
+            if b:
+                u(b - 1)
+            if b in fill:
+                fill[b]()
         u(3)
 
     def qsecond(c):
@@ -153,73 +152,61 @@ def rank_program(g, core, T, topo):
 
     quant("qb%d" % f1, [L["lb0"]], "qb", f1, "rb", f1 * W)
     for i in range(4):
-        quant("qa%d" % i, [L["la%d" % (i // 2)]], "qa", i, "ra", i * W)
+        quant("qa%d" % i, [L["la%d" % max(0, i - 1)]], "qa", i, "ra", i * W)
     quant("qb%d" % f2, [L["lb1"]], "qb", f2, "rb", f2 * W)
-    make("P", "v", f1, 3)
     qtile(f1)
-    for i in (0, 1):
-        make("P", "v", f2, i)
     quant("qbn", [L["lb2"]], "qb", near, "rb", near * W, 256)
-    qtile(f2)
-    second(f1)
-    qtile(x)
-    qsecond(f1)
-    second(f2)
-    qtile(own)
-    qsecond(f2)
-    second(x)
-    qsecond(x)
-    second(own)
+    second(f1, {2: lambda: qtile(f2)})
+    second(f2, {0: lambda: qsecond(f1), 2: lambda: qtile(x)})
+    second(x, {0: lambda: qsecond(f2), 1: lambda: qtile(own)})
+    second(own, {0: lambda: qsecond(x)})
     qsecond(own)
     for h in range(2):
         for b in range(4):
             add("v", "y%d_%d" % (h, b), ["UX_%d" % b, "dc%d" % b],
-                (lambda b, lo: lambda: g.vector.tensor_tensor(T.yo[:, 4 * lo + b:4 * lo + 256:4], bank("py", b, lo, 64), T.dc[:, b * NC + lo:b * NC + lo + 64], AluOpType.add))(b, 64 * h))
+                (lambda b, lo: lambda: g.vector.tensor_tensor(T.yo[:, 4 * lo + b:4 * lo + 256:4], bank("px", b, lo, 64), T.dc[:, b * NC + lo:b * NC + lo + 64], AluOpType.add))(b, 64 * h))
 
-    for i in (0, 1, 2):
-        make("P", "a", f1, i)
-    for i in range(4):
-        make("F", "a", f1, i, ["P%d_%d" % (f1, i)])
-    for i in (2, 3):
-        make("P", "a", f2, i)
-    for i in range(4):
-        make("F", "a", f2, i, ["P%d_%d" % (f2, i)])
-    for c in (x, own):
+    for c in order:
         for i in range(4):
-            make("P", "a", c, i)
+            make("P", c, i)
         for i in range(4):
-            make("F", "a", c, i)
+            make("F", c, i)
     for b in range(4):
-        add("a", "dc%d" % b, ["E%d_%d" % (own, b)], (lambda b: lambda: g.scalar.activation(T.dc[:, b * NC:(b + 1) * NC], bank("px", b), A.Copy))(b))
-
-    for i in range(4):
-        mm("Z1_%d" % i, ["qa%d" % i, "qb%d" % f1], bank("px", i), "qa", i, "qb", f1)
-    for i in range(4):
-        mm("Z2_%d" % i, ["qb%d" % f2], bank("py", i), "qa", i, "qb", f2)
+        add("a", "dc%d" % b, ["E%d_%d" % (own, b)], (lambda b: lambda: g.scalar.activation(T.dc[:, b * NC:(b + 1) * NC], bank(dbuf[own], b), A.Copy))(b))
 
     def held(c, free):
         for b in range(4):
-            mm("D%d_%d" % (c, b), ["S%d" % b, "q%d" % c] + [f % b for f in free], bank("px", b), "qs", b, "q", c)
+            mm("D%d_%d" % (c, b), ["S%d" % b, "q%d" % c] + [f % b for f in free], bank(dbuf[c], b), "qs", b, "q", c)
 
-    held(f1, ["F%d_%%d" % f1, "P%d_%%d" % f1])
-    for i in range(4):
-        mm("ZN_%d" % i, ["qbn", "F%d_%d" % (f2, i), "P%d_%d" % (f2, i)], bank("py", i, 0, 256), "qa", i, "qb", near, 256)
-    held(f2, ["E%d_%%d" % f1])
-    held(x, ["E%d_%%d" % f2])
-    held(own, ["E%d_%%d" % x])
+    def near_z(i):
+        mm("ZN_%d" % i, ["qbn", "E%d_%d" % (f1, i)], bank("px", i, 0, 256), "qa", i, "qb", near, 256)
 
     def total(src, what):
         m = plan(src, cores, topo)[1]
         return len(engines(m[(what, rank)])) + len(engines(m[(what + "_s", rank)]))
 
-    for j, src in enumerate((f1, f2, x)):
+    def first(src):
         for b in range(4):
-            mm("A%d_%d" % (j, b), [("aq%d" % src, total(src, "q"))] + ["%s%d_%d" % (k, c, b) for k in "PF" for c in (x, own)],
-               bank("py", b), "qs", b, "lq", src, start=(j == 0), stop=False)
+            mm("A%d_%d" % (src, b), [("aq%d" % src, total(src, "q"))] + ["%s%d_%d" % (k, c, b) for k in "PF" for c in (x, own)],
+               bank("px", b), "qs", b, "lq", src, start=(src == f1), stop=False)
+
+    for i in range(4):
+        mm("Z1_%d" % i, ["qa%d" % i, "qb%d" % f1], bank("px", i), "qa", i, "qb", f1)
+    for i in range(4):
+        mm("Z2_%d" % i, ["qb%d" % f2], bank("py", i), "qa", i, "qb", f2)
+    held(f1, ["F%d_%%d" % f1, "P%d_%%d" % f1])
+    for i in range(3):
+        near_z(i)
+    held(f2, ["F%d_%%d" % f2, "P%d_%%d" % f2])
+    near_z(3)
+    held(x, ["E%d_%%d" % f2])
+    held(own, ["E%d_%%d" % x])
+    for src in (f1, f2, x):
+        first(src)
     for src in (f1, f2, own, x):
         for b in range(4):
             dep = ["qu%d" % own] if src == own else [("au%d" % src, total(src, "u"))]
-            mm("UX_%d" % b if src == x else "U%d_%d" % (src, b), dep, bank("py", b), "qs", b, "qu" if src == own else "lu", src, start=False, stop=(src == x))
+            mm("UX_%d" % b if src == x else "U%d_%d" % (src, b), dep, bank("px", b), "qs", b, "qu" if src == own else "lu", src, start=False, stop=(src == x))
 
     sent = [0]
 
@@ -252,9 +239,11 @@ def rank_program(g, core, T, topo):
         add("g", None, deps, call, False)
 
     send(["q%d" % f1], [("q", f1)])
-    send(["q%d" % f2, "q%d" % x], [("q", f2), ("q", x)])
-    send([], [("q_s", f1), ("q_s", f2), ("q_s", x)])
-    for c in (f1, f2, x):
+    send(["q%d" % f2], [("q", f2)])
+    send([], [("q_s", f1), ("q_s", f2)])
+    send(["qu%d" % f1, "q%d" % x], [("u", f1), ("q", x)])
+    send([], [("u_s", f1), ("q_s", x)])
+    for c in (f2, x):
         send(["qu%d" % c], [("u", c)])
         send([], [("u_s", c)])
 

from concourse.bass import DstId, RemoteDMATransfer
from concourse.mybir import dt, AluOpType, ActivationFunctionType

C = 0.031
NC = 128
W = 4 * NC
CODES = "float8_e4m3fn_x4"

SCRATCH = {
    "one": ("sbuf", [128, 128], "bfloat16"),
    "pick": ("sbuf", [128, 520], "bfloat16"),
    "ra": ("sbuf", [128, 2048], "bfloat16"),
    "rb": ("sbuf", [128, 2048], "bfloat16"),
    "rg": ("sbuf", [128, 2048], "bfloat16"),
    "t": ("sbuf", [128, 2048], "bfloat16"),
    "u": ("sbuf", [128, 2048], "bfloat16"),
    "rf": ("sbuf", [128, 2048], "float32"),
    "ef": ("sbuf", [128, 2048], "float32"),
    "dc": ("sbuf", [128, 512], "float32"),
    "yo": ("sbuf", [128, 512], "float32"),
    "px": ("psum", [128, 2048], "float32"),
    "py": ("psum", [128, 2048], "float32"),
}
for _n in ("qs", "qa", "qb", "q", "qu", "lq", "lu"):
    SCRATCH[_n] = ("sbuf", [128, 512], CODES)
    SCRATCH[_n + "_s"] = ("sbuf", [128, 512], "uint8")

LOADS = ["la0", "la1", "la2", "lb0", "lb1", "lb2", "lg0", "lg1", "lg2"]
SEMAPHORES = LOADS + ["sv", "sa", "sp", "sg", "sent", "sy0", "sy1"] + ["aq%d" % r for r in range(4)] + ["au%d" % r for r in range(4)]


def engines(m):
    return [e for e in range(m.bit_length()) if (m >> e) & 1]


def mask_of(es):
    return sum(1 << e for e in es)


def plan(rank, cores, topo):
    me = cores[rank]
    others = [c for c in range(len(cores)) if c != rank]
    others.sort(key=lambda c: (topo.chip(cores[c]) == topo.chip(me), topo.die(cores[c]) != topo.die(me)))
    f1, f2, x = others
    off = engines(topo.mask(me, cores[f1]))
    on = engines(topo.mask(me, cores[x]))
    rest = [e for e in on if e not in off]
    h = len(off) // 2
    m = {("q", f1): off, ("q", f2): off, ("q", x): rest,
         ("q_s", f1): off[:h], ("q_s", f2): off[h:], ("q_s", x): rest,
         ("u", f1): off, ("u", f2): off, ("u", x): on,
         ("u_s", f1): off, ("u_s", f2): off, ("u_s", x): on}
    return others + [rank], {k: mask_of(v) for k, v in m.items()}


def rank_program(g, core, T, topo):
    rank = T.rank_of(core)
    if rank is None:
        return
    cores = list(T.cores)
    order, masks = plan(rank, cores, topo)
    f1, f2, x, own = order
    S = T.sem
    A = ActivationFunctionType
    queues = {"v": g.vector, "a": g.scalar, "t": g.tensor, "g": g, "s": g.sync}
    counter = {"v": "sv", "a": "sa", "t": "sp"}
    ops = {k: [] for k in queues}
    at = {}
    count = {k: 0 for k in queues}

    def add(eng, label, deps, call, counted=True):
        if counted:
            count[eng] += 1
            at[label] = (counter[eng], count[eng])
        ops[eng].append((deps, call, counted))

    def codes(buf, c, n=NC):
        return T[buf][:, c * NC:c * NC + n]

    def plane(buf, c, n=NC):
        return T[buf + "_s"][:, c * NC:c * NC + n]

    def bank(buf, b, off=0, n=NC):
        return T[buf][:, b * 512 + off:b * 512 + off + n]

    def comb(buf, c, b):
        return T[buf][:, c * W + b:(c + 1) * W:4]

    def flat(buf, c, b):
        return T[buf][:, c * W + b * NC:c * W + (b + 1) * NC]

    near = min(x, own)

    def load(eng, sem, dst, src, lo, n=W):
        add(eng, None, [], lambda: queues[eng].dma_start(dst[:, lo:lo + n], src[:, lo:lo + n]).then_inc(S[sem], 16), False)

    load("s", "lb0", T.rb, T.b, f1 * W)
    load("a", "la0", T.ra, T.a, 0, 2 * W)
    load("s", "la1", T.ra, T.a, 2 * W)
    load("a", "la2", T.ra, T.a, 3 * W)
    load("s", "lb1", T.rb, T.b, f2 * W)
    load("s", "lb2", T.rb, T.b, near * W, 2 * W)
    load("s", "lg0", T.rg, T.gr, f1 * W)
    load("s", "lg2", T.rg, T.gr, f2 * W)
    load("s", "lg1", T.rg, T.gr, near * W, 2 * W)
    L = {k: (k, 16) for k in LOADS}
    gload = {f1: L["lg0"], f2: L["lg2"], x: L["lg1"], own: L["lg1"]}

    add("v", "one", [], lambda: g.vector.memset(T.one[:], 1.0))
    add("v", "zero", [], lambda: g.vector.memset(T.pick[:, 0:520], 0.0))
    add("g", None, ["zero"], lambda: g.affine_select(T.pick[:, 3:515:4], T.one[:], [[-1, 128]], AluOpType.is_equal, 0.0, 0, 1).then_inc(S.sg, 1), False)

    def quant(label, deps, buf, c, src, lo, n=NC):
        add("v", label, deps, lambda: g.vector.quantize_mx(codes(buf, c, n), plane(buf, c, n), T[src][:, lo:lo + 4 * n]))

    for b in range(4):
        quant("S%d" % b, [("sg", 1)], "qs", b, "pick", 3 - b)

    def mm(label, deps, out, w, i, m, c, n=NC, start=True, stop=True):
        add("t", label, deps, lambda: g.tensor.matmul_mx(out, codes(w, i), plane(w, i), codes(m, c, n), plane(m, c, n), start, stop))

    zbuf = {f1: ("px", 0), f2: ("py", 0), x: ("px", (x - near) * NC), own: ("px", (own - near) * NC)}
    zlab = {f1: "Z1_%d", f2: "Z2_%d", x: "ZN_%d", own: "ZN_%d"}
    dbuf = {f1: "px", f2: "py", x: "py", own: "py"}

    def make(which, c, i):
        out = comb("t", c, i) if which == "P" else flat("rf", c, i)
        add("a", "%s%d_%d" % (which, c, i), [zlab[c] % i], lambda: g.scalar.activation(out, bank(zbuf[c][0], i, zbuf[c][1]), A.Relu, scale=C))

    def qtile(c):
        quant("q%d" % c, ["P%d_%d" % (c, i) for i in range(4)], "q", c, "t", c * W)

    def second(c, fill):
        def e(b):
            add("v", "E%d_%d" % (c, b), ["D%d_%d" % (c, b), "F%d_%d" % (c, b)],
                lambda: g.vector.tensor_tensor(flat("ef", c, b), flat("rf", c, b), bank(dbuf[c], b), AluOpType.subtract))

        def u(b):
            add("v", "u%d_%d" % (c, b), ["E%d_%d" % (c, b), gload[c]],
                lambda: g.vector.tensor_tensor(comb("u", c, b), comb("rg", c, b), flat("ef", c, b), AluOpType.add))

        for b in range(4):
            e(b)
            if b:
                u(b - 1)
            if b in fill:
                fill[b]()
        u(3)

    def qsecond(c):
        quant("qu%d" % c, ["u%d_%d" % (c, b) for b in range(4)], "qu", c, "u", c * W)

    quant("qb%d" % f1, [L["lb0"]], "qb", f1, "rb", f1 * W)
    for i in range(4):
        quant("qa%d" % i, [L["la%d" % max(0, i - 1)]], "qa", i, "ra", i * W)
    quant("qb%d" % f2, [L["lb1"]], "qb", f2, "rb", f2 * W)
    qtile(f1)
    quant("qbn", [L["lb2"]], "qb", near, "rb", near * W, 256)
    second(f1, {2: lambda: qtile(f2)})
    second(f2, {0: lambda: qsecond(f1), 2: lambda: qtile(x)})
    second(x, {0: lambda: qsecond(f2), 1: lambda: qtile(own)})
    second(own, {0: lambda: qsecond(x)})
    qsecond(own)
    for h in range(2):
        for b in range(4):
            add("v", "y%d_%d" % (h, b), ["UX_%d" % b, "dc%d" % b],
                (lambda b, lo: lambda: g.vector.tensor_tensor(T.yo[:, 4 * lo + b:4 * lo + 256:4], bank("px", b, lo, 64), T.dc[:, b * NC + lo:b * NC + lo + 64], AluOpType.add))(b, 64 * h))

    for c in order:
        for i in range(4):
            make("P", c, i)
        for i in range(4):
            make("F", c, i)
    for b in range(4):
        add("a", "dc%d" % b, ["E%d_%d" % (own, b)], (lambda b: lambda: g.scalar.activation(T.dc[:, b * NC:(b + 1) * NC], bank(dbuf[own], b), A.Copy))(b))

    def held(c, free):
        for b in range(4):
            mm("D%d_%d" % (c, b), ["S%d" % b, "q%d" % c] + [f % b for f in free], bank(dbuf[c], b), "qs", b, "q", c)

    def near_z(i):
        mm("ZN_%d" % i, ["qbn", "E%d_%d" % (f1, i)], bank("px", i, 0, 256), "qa", i, "qb", near, 256)

    def total(src, what):
        m = plan(src, cores, topo)[1]
        return len(engines(m[(what, rank)])) + len(engines(m[(what + "_s", rank)]))

    def first(src):
        for b in range(4):
            mm("A%d_%d" % (src, b), [("aq%d" % src, total(src, "q"))] + ["%s%d_%d" % (k, c, b) for k in "PF" for c in (x, own)],
               bank("px", b), "qs", b, "lq", src, start=(src == f1), stop=False)

    for i in range(4):
        mm("Z1_%d" % i, ["qa%d" % i, "qb%d" % f1], bank("px", i), "qa", i, "qb", f1)
    for i in range(4):
        mm("Z2_%d" % i, ["qb%d" % f2], bank("py", i), "qa", i, "qb", f2)
    held(f1, ["F%d_%%d" % f1, "P%d_%%d" % f1])
    for i in range(3):
        near_z(i)
    held(f2, ["F%d_%%d" % f2, "P%d_%%d" % f2])
    near_z(3)
    held(x, ["E%d_%%d" % f2])
    held(own, ["E%d_%%d" % x])
    for src in (f1, f2, x):
        first(src)
    for src in (f1, f2, own, x):
        for b in range(4):
            dep = ["qu%d" % own] if src == own else [("au%d" % src, total(src, "u"))]
            mm("UX_%d" % b if src == x else "U%d_%d" % (src, b), dep, bank("px", b), "qs", b, "qu" if src == own else "lu", src, start=False, stop=(src == x))

    sent = [0]

    def dest(c):
        rid, pid, _se = topo.addr(cores[c])
        return rid, pid

    def piece(kind, c):
        src = {"q": "q", "u": "qu"}[kind[0]]
        land = {"q": "lq", "u": "lu"}[kind[0]]
        if kind.endswith("_s"):
            return plane(src, c), plane(land, rank)
        return codes(src, c).bitcast(dt.uint8), codes(land, rank).bitcast(dt.uint8)

    def send(deps, items):
        def call():
            tr = []
            for kind, c in items:
                rid, pid = dest(c)
                s, d = piece(kind, c)
                tr.append((rid, pid, s, d, masks[(kind, c)], S["a%s%d" % (kind[0], rank)]))
            if len(tr) == 1:
                rid, pid, s, d, m, sem = tr[0]
                g.remote_dma(d, s, sem, S.sent, pid, rid, m)
            else:
                g.remote_dma_fused([RemoteDMATransfer(dst_ids=[DstId(rid=rid, pnc=pid)], dma_engine_mask=m, remote_sem=sem, src=s, dst=d)
                                    for rid, pid, s, d, m, sem in tr], local_sem=S.sent)
        for kind, c in items:
            sent[0] += len(engines(masks[(kind, c)]))
        add("g", None, deps, call, False)

    send(["q%d" % f1], [("q", f1)])
    send(["q%d" % f2], [("q", f2)])
    send([], [("q_s", f1), ("q_s", f2)])
    send(["qu%d" % f1, "q%d" % x], [("u", f1), ("q", x)])
    send([], [("u_s", f1), ("q_s", x)])
    for c in (f2, x):
        send(["qu%d" % c], [("u", c)])
        send([], [("u_s", c)])

    for h in range(2):
        add("s", None, ["y%d_%d" % (h, b) for b in range(4)],
            (lambda h: lambda: g.sync.dma_start(T.y[:, 256 * h:256 * h + 256], T.yo[:, 256 * h:256 * h + 256]).then_inc(S["sy%d" % h], 16))(h), False)

    for eng in ops:
        q = queues[eng]
        seen = {}
        for deps, call, counted in ops[eng]:
            need = {}
            for d in deps:
                s, n = at[d] if isinstance(d, str) else d
                need[s] = max(need.get(s, 0), n)
            for s, n in need.items():
                if seen.get(s, 0) < n:
                    q.wait_ge(S[s], n)
                    seen[s] = n
            ins = call()
            if counted:
                ins.then_inc(S[counter[eng]], 1)
    g.sync.wait_ge(S.sy0, 16)
    g.sync.wait_ge(S.sy1, 16)
    g.wait_ge(S.sent, sent[0])
